import numpy as np, ml_dtypes
CORES = [49,52,55,57,60,63,65,68,71,73,76,79]
N = 12
F = 64
BETA, LR = 0.75, 0.5
def setup_inputs(rng):
    return {"gr": rng.standard_normal((N, 128, N * F), dtype=np.float32).astype(ml_dtypes.bfloat16), "m": rng.standard_normal((N, 128, F), dtype=np.float32).astype(ml_dtypes.bfloat16), "w": rng.standard_normal((N, 128, F), dtype=np.float32).astype(ml_dtypes.bfloat16)}
def setup_inputs_big(rng):
    d = setup_inputs(rng)
    for k in ("gr", "m", "w"): d[k] = (d[k].astype(np.float32) * 1048576.0).astype(d[k].dtype)
    return d
def setup_inputs_small(rng):
    d = setup_inputs(rng)
    for k in ("gr", "m", "w"): d[k] = (d[k].astype(np.float32) * (1 / 1048576.0)).astype(d[k].dtype)
    return d
def setup_inputs_apart(rng):
    d = setup_inputs(rng)
    f = (10.0 ** rng.permutation(np.linspace(-1.5, 1.5, N))).astype(np.float32).reshape(N, 1, 1)
    for k in ("gr", "m", "w"): d[k] = (d[k].astype(np.float32) * f).astype(d[k].dtype)
    return d
def reference(gr, m, w):
    GR, M, W = gr.astype(np.float64), m.astype(np.float64), w.astype(np.float64)
    s = GR.sum(axis=0)
    m2 = np.stack([BETA * M[r] + s[:, F * r:F * r + F] for r in range(N)])
    w2 = np.concatenate([W[r] - LR * m2[r] for r in range(N)], axis=1)
    return {"y": np.broadcast_to(w2.astype(ml_dtypes.bfloat16), (N, 128, N * F)), "mo": m2.astype(ml_dtypes.bfloat16)}

@@ -1,0 +1,141 @@
+from concourse.bass import DstId, RemoteDMATransfer
+from concourse.mybir import AluOpType
+
+N = 12
+F = 64
+NSIM = 80
+NP = 3
+PW = N * F // NP
+NE1 = 4
+NE2 = 8
+NE3 = 8
+
+SCRATCH = {
+    "G": ("sbuf", [128, N * F], "bfloat16"),
+    "Mt": ("sbuf", [128, F], "bfloat16"),
+    "Wt": ("sbuf", [128, F], "bfloat16"),
+    "K75": ("sbuf", [128, F], "bfloat16"),
+    "Km2": ("sbuf", [128, F], "bfloat16"),
+    "Cm": ("sbuf", [128, PW], "bfloat16"),
+    "Cw": ("sbuf", [128, PW], "bfloat16"),
+    "Kh": ("psum", [128, PW], "float32"),
+    "S": ("sbuf", [128, N * F], "bfloat16"),
+    "Y": ("sbuf", [128, N * F], "bfloat16"),
+    "MO": ("sbuf", [128, F], "bfloat16"),
+    "A": ("dram", [3, 128, PW], "bfloat16"),
+    "B": ("dram", [4, 128, PW], "bfloat16"),
+}
+SEMAPHORES = ["s_g", "s_mw", "s_v", "s_c", "s_a", "s_b", "s_l", "s_s0", "s_s1", "s_s2", "s_s3", "s_y", "s_mo", "s_st"]
+
+
+def _bits(mask):
+    return [e for e in range(16) if (mask >> e) & 1]
+
+
+def _mask(engines):
+    m = 0
+    for e in engines:
+        m |= 1 << e
+    return m
+
+
+def _common(topo, src, dsts):
+    m = topo.mask(src, dsts[0])
+    for d in dsts[1:]:
+        m &= topo.mask(src, d)
+    return _bits(m)
+
+
+def _dst(topo, c):
+    a = topo.addr(c)
+    return DstId(rid=a[0], pnc=a[1])
+
+
+def rank_program(g, core, T, topo):
+    cores = list(T.cores)
+    chips = sorted(set(topo.chip(c) for c in cores))
+    my_chip = topo.chip(core)
+    if my_chip not in chips:
+        return
+    ci = chips.index(my_chip)
+
+    def leaders_of(ch):
+        out = []
+        for c in range(NSIM):
+            if topo.chip(c) == ch and T.rank_of(c) is None and all(topo.may_write(c, r) for r in cores):
+                out.append(c)
+        return out[:NP]
+
+    def ranks_of(ch):
+        return [c for c in cores if topo.chip(c) == ch]
+
+    leaders = leaders_of(my_chip)
+    ranks = ranks_of(my_chip)
+    sem = T.sem
+    s_s = [sem["s_s%d" % k] for k in range(NP)]
+    rank = T.rank_of(core)
+
+    if rank is None:
+        if core not in leaders:
+            return
+        k = leaders.index(core)
+        peers = [leaders_of(ch)[k] for ch in chips if ch != my_chip]
+        mine = [T.A[j] for j in range(len(ranks))]
+        g.wait_ge(sem.s_a, NE1 * len(ranks))
+        e2 = _common(topo, core, peers)[:NE2]
+        g.remote_dma_fused([RemoteDMATransfer(
+            dst_ids=[_dst(topo, p) for p in peers], dma_engine_mask=_mask(e2), remote_sem=sem.s_b,
+            srcs=mine, dsts=[T.B[ci] for p in peers], alu_op=1)], local_sem=sem.s_l)
+        g.wait_ge(sem.s_b, NE2 * len(peers))
+        e3 = _common(topo, core, ranks)[:NE3]
+        g.remote_dma_fused([RemoteDMATransfer(
+            dst_ids=[_dst(topo, r) for r in ranks], dma_engine_mask=_mask(e3), remote_sem=s_s[k],
+            srcs=mine + [T.B[x] for x in range(len(chips)) if x != ci],
+            dsts=[T.S[:, k * PW:(k + 1) * PW] for r in ranks], alu_op=1)], local_sem=sem.s_l)
+        g.wait_ge(sem.s_l, NE2 + NE3)
+        return
+
+    v = g.vector
+    slot = ranks.index(core)
+    kp = (rank * F) // PW
+    off = rank * F - kp * PW
+    g.sync.dma_start(T.G[:], T.gr[:]).then_inc(sem.s_g, 16)
+    g.scalar.dma_start(T.Mt[:], T.m[:]).then_inc(sem.s_mw, 16)
+    g.scalar.dma_start(T.Wt[:], T.w[:]).then_inc(sem.s_mw, 16)
+    v.memset(T.K75[:], 0.75).then_inc(sem.s_v, 1)
+    v.memset(T.Km2[:], -2.0).then_inc(sem.s_v, 1)
+    v.memset(T.Cm[:], 0.0).then_inc(sem.s_v, 1)
+    v.memset(T.Cw[:], 0.0).then_inc(sem.s_v, 1)
+    v.memset(T.Kh[:], -0.5).then_inc(sem.s_v, 1)
+    v.wait_ge(sem.s_v, 5)
+    v.wait_ge(sem.s_mw, 32)
+    v.tensor_tensor(T.Cm[:, off:off + F], T.Mt[:], T.K75[:], AluOpType.mult).then_inc(sem.s_c, 1)
+    v.tensor_tensor(T.Cw[:, off:off + F], T.Wt[:], T.Km2[:], AluOpType.mult).then_inc(sem.s_c, 1)
+
+    eng = _common(topo, core, leaders)
+    order = eng[0::2] + eng[1::2]
+    seq = sorted(range(NP), key=lambda k: (topo.die(leaders[k]) == topo.die(core), k))
+    trs = []
+    for n, k in enumerate(seq):
+        srcs = [T.G[:, k * PW:(k + 1) * PW]]
+        if k == kp:
+            srcs = srcs + [T.Cm[:], T.Cw[:]]
+        trs.append(RemoteDMATransfer(
+            dst_ids=[_dst(topo, leaders[k])], dma_engine_mask=_mask(order[n * NE1:(n + 1) * NE1]), remote_sem=sem.s_a,
+            srcs=srcs, dsts=[T.A[slot]], alu_op=1 if k == kp else 0))
+    g.wait_ge(sem.s_g, 16)
+    g.wait_ge(sem.s_c, 2)
+    g.remote_dma_fused(trs, local_sem=sem.s_l)
+
+    v.wait_ge(sem.s_c, 2)
+    for k in range(NP):
+        v.wait_ge(s_s[k], NE3)
+        v.tensor_tensor(T.Y[:, k * PW:(k + 1) * PW], T.S[:, k * PW:(k + 1) * PW], T.Kh[:], AluOpType.mult).then_inc(sem.s_y, 1)
+        if k == kp:
+            v.tensor_tensor(T.MO[:], T.S[:, rank * F:(rank + 1) * F], T.Cw[:, off:off + F], AluOpType.subtract).then_inc(sem.s_mo, 1)
+    g.sync.wait_ge(sem.s_y, NP)
+    g.sync.dma_start(T.y[:], T.Y[:]).then_inc(sem.s_st, 16)
+    g.scalar.wait_ge(sem.s_mo, 1)
+    g.scalar.dma_start(T.mo[:], T.MO[:]).then_inc(sem.s_st, 16)
+    g.wait_ge(sem.s_l, NE1 * NP)
+    g.wait_ge(sem.s_st, 32)

@@ -4,11 +4,11 @@ from concourse.mybir import AluOpType
 N = 12
 F = 64
 NSIM = 80
-NP = 3
+NP = 4
 PW = N * F // NP
 NE1 = 4
 NE2 = 8
-NE3 = 8
+NE3 = 16
 
 SCRATCH = {
     "G": ("sbuf", [128, N * F], "bfloat16"),
@@ -24,8 +24,10 @@ SCRATCH = {
     "MO": ("sbuf", [128, F], "bfloat16"),
     "A": ("dram", [3, 128, PW], "bfloat16"),
     "B": ("dram", [4, 128, PW], "bfloat16"),
+    "Cd": ("dram", [2, 128, PW], "bfloat16"),
 }
-SEMAPHORES = ["s_g", "s_mw", "s_v", "s_c", "s_a", "s_b", "s_l", "s_s0", "s_s1", "s_s2", "s_s3", "s_y", "s_mo", "s_st"]
+SEMAPHORES = ["s_g", "s_mw", "s_v", "s_c", "s_a", "s_b", "s_l", "s_s0", "s_s1", "s_s2", "s_s3", "s_y", "s_mo", "s_st",
+              "s_o"]
 
 
 def _bits(mask):
@@ -59,49 +61,74 @@ def rank_program(g, core, T, topo):
         return
     ci = chips.index(my_chip)
 
-    def leaders_of(ch):
+    def senders_of(ch):
+        return [c for c in range(NSIM) if topo.chip(c) == ch and all(topo.may_write(c, r) for r in cores)][:NP]
+
+    def finishers_of(ch):
+        snd = senders_of(ch)
         out = []
-        for c in range(NSIM):
-            if topo.chip(c) == ch and T.rank_of(c) is None and all(topo.may_write(c, r) for r in cores):
+        for c in snd:
+            if T.rank_of(c) is None:
                 out.append(c)
-        return out[:NP]
+            else:
+                out.append([h for h in range(NSIM) if topo.chip(h) == ch and T.rank_of(h) is None
+                            and h not in snd and h not in out and topo.die(h) == topo.die(c)][0])
+        return out
 
-    def ranks_of(ch):
-        return [c for c in cores if topo.chip(c) == ch]
-
-    leaders = leaders_of(my_chip)
-    ranks = ranks_of(my_chip)
+    snd = senders_of(my_chip)
+    fin = finishers_of(my_chip)
+    ranks = [c for c in cores if topo.chip(c) == my_chip]
+    others = [ch for ch in chips if ch != my_chip]
     sem = T.sem
     s_s = [sem["s_s%d" % k] for k in range(NP)]
     rank = T.rank_of(core)
+    mine = [T.A[j] for j in range(len(ranks))]
 
-    if rank is None:
-        if core not in leaders:
-            return
-        k = leaders.index(core)
-        peers = [leaders_of(ch)[k] for ch in chips if ch != my_chip]
-        mine = [T.A[j] for j in range(len(ranks))]
-        g.wait_ge(sem.s_a, NE1 * len(ranks))
-        e2 = _common(topo, core, peers)[:NE2]
-        g.remote_dma_fused([RemoteDMATransfer(
-            dst_ids=[_dst(topo, p) for p in peers], dma_engine_mask=_mask(e2), remote_sem=sem.s_b,
-            srcs=mine, dsts=[T.B[ci] for p in peers], alu_op=1)], local_sem=sem.s_l)
-        g.wait_ge(sem.s_b, NE2 * len(peers))
+    def hop3(k, srcs):
         e3 = _common(topo, core, ranks)[:NE3]
         g.remote_dma_fused([RemoteDMATransfer(
             dst_ids=[_dst(topo, r) for r in ranks], dma_engine_mask=_mask(e3), remote_sem=s_s[k],
-            srcs=mine + [T.B[x] for x in range(len(chips)) if x != ci],
-            dsts=[T.S[:, k * PW:(k + 1) * PW] for r in ranks], alu_op=1)], local_sem=sem.s_l)
-        g.wait_ge(sem.s_l, NE2 + NE3)
+            srcs=srcs, dsts=[T.S[:, k * PW:(k + 1) * PW] for r in ranks], alu_op=1)], local_sem=sem.s_l)
+
+    if rank is None:
+        if core in snd:
+            k = snd.index(core)
+            peers = [finishers_of(ch)[k] for ch in others]
+            g.wait_ge(sem.s_a, NE1 * len(ranks))
+            e2 = _common(topo, core, peers)[:NE2]
+            g.remote_dma_fused([RemoteDMATransfer(
+                dst_ids=[_dst(topo, p) for p in peers], dma_engine_mask=_mask(e2), remote_sem=sem.s_b,
+                srcs=mine, dsts=[T.B[ci] for p in peers], alu_op=1)], local_sem=sem.s_l)
+            g.wait_ge(sem.s_b, NE2 * len(peers))
+            hop3(k, mine + [T.B[x] for x in range(len(chips)) if x != ci])
+            g.wait_ge(sem.s_l, NE2 + NE3)
+        elif core in fin:
+            k = fin.index(core)
+            g.wait_ge(sem.s_b, NE2 * len(chips))
+            hop3(k, [T.B[x] for x in range(len(chips))])
+            g.wait_ge(sem.s_l, NE3)
         return
 
     v = g.vector
     slot = ranks.index(core)
     kp = (rank * F) // PW
     off = rank * F - kp * PW
-    g.sync.dma_start(T.G[:], T.gr[:]).then_inc(sem.s_g, 16)
+    ko = snd.index(core) if core in snd else None
+    out1 = [k for k in range(NP) if k != ko]
+    runs = []
+    for k in out1:
+        if runs and runs[-1][1] == k:
+            runs[-1][1] = k + 1
+        else:
+            runs.append([k, k + 1])
+    for a, b in runs:
+        g.sync.dma_start(T.G[:, a * PW:b * PW], T.gr[:, a * PW:b * PW]).then_inc(sem.s_g, 16)
     g.scalar.dma_start(T.Mt[:], T.m[:]).then_inc(sem.s_mw, 16)
     g.scalar.dma_start(T.Wt[:], T.w[:]).then_inc(sem.s_mw, 16)
+    n_o = 0
+    if ko is not None:
+        g.scalar.dma_start(T.A[slot], T.gr[:, ko * PW:(ko + 1) * PW]).then_inc(sem.s_o, 16)
+        n_o += 16
     v.memset(T.K75[:], 0.75).then_inc(sem.s_v, 1)
     v.memset(T.Km2[:], -2.0).then_inc(sem.s_v, 1)
     v.memset(T.Cm[:], 0.0).then_inc(sem.s_v, 1)
@@ -111,21 +138,41 @@ def rank_program(g, core, T, topo):
     v.wait_ge(sem.s_mw, 32)
     v.tensor_tensor(T.Cm[:, off:off + F], T.Mt[:], T.K75[:], AluOpType.mult).then_inc(sem.s_c, 1)
     v.tensor_tensor(T.Cw[:, off:off + F], T.Wt[:], T.Km2[:], AluOpType.mult).then_inc(sem.s_c, 1)
+    if ko is not None and ko == kp:
+        g.scalar.wait_ge(sem.s_c, 2)
+        g.scalar.dma_start(T.Cd[0], T.Cm[:]).then_inc(sem.s_o, 16)
+        g.scalar.dma_start(T.Cd[1], T.Cw[:]).then_inc(sem.s_o, 16)
+        n_o += 32
 
-    eng = _common(topo, core, leaders)
+    eng = _common(topo, core, [snd[k] for k in out1])
     order = eng[0::2] + eng[1::2]
-    seq = sorted(range(NP), key=lambda k: (topo.die(leaders[k]) == topo.die(core), k))
+    seq = sorted(out1, key=lambda k: (topo.die(snd[k]) == topo.die(core), k))
     trs = []
     for n, k in enumerate(seq):
         srcs = [T.G[:, k * PW:(k + 1) * PW]]
         if k == kp:
             srcs = srcs + [T.Cm[:], T.Cw[:]]
         trs.append(RemoteDMATransfer(
-            dst_ids=[_dst(topo, leaders[k])], dma_engine_mask=_mask(order[n * NE1:(n + 1) * NE1]), remote_sem=sem.s_a,
+            dst_ids=[_dst(topo, snd[k])], dma_engine_mask=_mask(order[n * NE1:(n + 1) * NE1]), remote_sem=sem.s_a,
             srcs=srcs, dsts=[T.A[slot]], alu_op=1 if k == kp else 0))
-    g.wait_ge(sem.s_g, 16)
+    g.wait_ge(sem.s_g, 16 * len(runs))
     g.wait_ge(sem.s_c, 2)
     g.remote_dma_fused(trs, local_sem=sem.s_l)
+    n_l = NE1 * len(trs)
+
+    if ko is not None:
+        peers = [finishers_of(ch)[ko] for ch in others]
+        srcs = mine + ([T.Cd[0], T.Cd[1]] if ko == kp else [])
+        e_off = _common(topo, core, peers)[:NE2]
+        e_on = [e for e in _bits(topo.mask(core, fin[ko])) if e not in e_off][:NE2]
+        g.wait_ge(sem.s_a, NE1 * (len(ranks) - 1))
+        g.wait_ge(sem.s_o, n_o)
+        g.remote_dma_fused([
+            RemoteDMATransfer(dst_ids=[_dst(topo, p) for p in peers], dma_engine_mask=_mask(e_off), remote_sem=sem.s_b,
+                              srcs=srcs, dsts=[T.B[ci] for p in peers], alu_op=1),
+            RemoteDMATransfer(dst_ids=[_dst(topo, fin[ko])], dma_engine_mask=_mask(e_on), remote_sem=sem.s_b,
+                              srcs=srcs, dsts=[T.B[ci]], alu_op=1)], local_sem=sem.s_l)
+        n_l += 2 * NE2
 
     v.wait_ge(sem.s_c, 2)
     for k in range(NP):
@@ -137,5 +184,5 @@ def rank_program(g, core, T, topo):
     g.sync.dma_start(T.y[:], T.Y[:]).then_inc(sem.s_st, 16)
     g.scalar.wait_ge(sem.s_mo, 1)
     g.scalar.dma_start(T.mo[:], T.MO[:]).then_inc(sem.s_st, 16)
-    g.wait_ge(sem.s_l, NE1 * NP)
+    g.wait_ge(sem.s_l, n_l)
     g.wait_ge(sem.s_st, 32)

@@ -6,28 +6,33 @@ F = 64
 NSIM = 80
 NP = 4
 PW = N * F // NP
-NE1 = 4
+NH = 2
+PH = NP // NH
+HW = PW * PH
+NE1 = 8
 NE2 = 8
 NE3 = 16
 
 SCRATCH = {
     "G": ("sbuf", [128, N * F], "bfloat16"),
+    "Z": ("sbuf", [128, N * F], "bfloat16"),
     "Mt": ("sbuf", [128, F], "bfloat16"),
     "Wt": ("sbuf", [128, F], "bfloat16"),
-    "K75": ("sbuf", [128, F], "bfloat16"),
-    "Km2": ("sbuf", [128, F], "bfloat16"),
+    "Km": ("sbuf", [128, F], "bfloat16"),
+    "Kw": ("sbuf", [128, F], "bfloat16"),
     "Cm": ("sbuf", [128, PW], "bfloat16"),
     "Cw": ("sbuf", [128, PW], "bfloat16"),
-    "Kh": ("psum", [128, PW], "float32"),
+    "Kh": ("psum", [128, HW], "float32"),
     "S": ("sbuf", [128, N * F], "bfloat16"),
-    "Y": ("sbuf", [128, N * F], "bfloat16"),
+    "Y": ("sbuf", [128, HW], "bfloat16"),
+    "D": ("sbuf", [128, F], "float32"),
     "MO": ("sbuf", [128, F], "bfloat16"),
     "A": ("dram", [3, 128, PW], "bfloat16"),
     "B": ("dram", [4, 128, PW], "bfloat16"),
     "Cd": ("dram", [2, 128, PW], "bfloat16"),
 }
-SEMAPHORES = ["s_g", "s_mw", "s_v", "s_c", "s_a", "s_b", "s_l", "s_s0", "s_s1", "s_s2", "s_s3", "s_y", "s_mo", "s_st",
-              "s_o"]
+SEMAPHORES = ["s_g0", "s_g1", "s_mw", "s_v", "s_c", "s_z", "s_a", "s_b", "s_l", "s_s0", "s_s1", "s_y", "s_d", "s_mo",
+              "s_st", "s_o"]
 
 
 def _bits(mask):
@@ -62,7 +67,18 @@ def rank_program(g, core, T, topo):
     ci = chips.index(my_chip)
 
     def senders_of(ch):
-        return [c for c in range(NSIM) if topo.chip(c) == ch and all(topo.may_write(c, r) for r in cores)][:NP]
+        ports = [c for c in range(NSIM) if topo.chip(c) == ch and all(topo.may_write(c, r) for r in cores)]
+        dies = []
+        for c in ports:
+            if topo.die(c) not in dies:
+                dies.append(topo.die(c))
+        groups = [[c for c in ports if topo.die(c) == d] for d in dies]
+        out = []
+        for i in range(max(len(q) for q in groups)):
+            for q in groups:
+                if i < len(q):
+                    out.append(q[i])
+        return out[:NP]
 
     def finishers_of(ch):
         snd = senders_of(ch)
@@ -80,14 +96,14 @@ def rank_program(g, core, T, topo):
     ranks = [c for c in cores if topo.chip(c) == my_chip]
     others = [ch for ch in chips if ch != my_chip]
     sem = T.sem
-    s_s = [sem["s_s%d" % k] for k in range(NP)]
+    s_s = [sem["s_s%d" % h] for h in range(NH)]
     rank = T.rank_of(core)
     mine = [T.A[j] for j in range(len(ranks))]
 
     def hop3(k, srcs):
         e3 = _common(topo, core, ranks)[:NE3]
         g.remote_dma_fused([RemoteDMATransfer(
-            dst_ids=[_dst(topo, r) for r in ranks], dma_engine_mask=_mask(e3), remote_sem=s_s[k],
+            dst_ids=[_dst(topo, r) for r in ranks], dma_engine_mask=_mask(e3), remote_sem=s_s[k // PH],
             srcs=srcs, dsts=[T.S[:, k * PW:(k + 1) * PW] for r in ranks], alu_op=1)], local_sem=sem.s_l)
 
     if rank is None:
@@ -113,52 +129,77 @@ def rank_program(g, core, T, topo):
     slot = ranks.index(core)
     kp = (rank * F) // PW
     off = rank * F - kp * PW
+    hk = kp // PH
     ko = snd.index(core) if core in snd else None
-    out1 = [k for k in range(NP) if k != ko]
-    runs = []
-    for k in out1:
-        if runs and runs[-1][1] == k:
-            runs[-1][1] = k + 1
-        else:
-            runs.append([k, k + 1])
-    for a, b in runs:
-        g.sync.dma_start(T.G[:, a * PW:b * PW], T.gr[:, a * PW:b * PW]).then_inc(sem.s_g, 16)
+    blk = T.S[:, rank * F:(rank + 1) * F]
+
+    g.sync.dma_start(T.G[:, 0:HW], T.gr[:, 0:HW]).then_inc(sem.s_g0, 16)
     g.scalar.dma_start(T.Mt[:], T.m[:]).then_inc(sem.s_mw, 16)
-    g.scalar.dma_start(T.Wt[:], T.w[:]).then_inc(sem.s_mw, 16)
+    g.scalar.dma_start(T.Wt[:] if hk == 0 else T.Cw[:, off:off + F], T.w[:]).then_inc(sem.s_mw, 16)
+    g.scalar.dma_start(T.G[:, HW:2 * HW], T.gr[:, HW:2 * HW]).then_inc(sem.s_g1, 16)
+
+    n_v = 3
+    v.memset(T.Km[:], 0.75 if hk == 0 else -0.375).then_inc(sem.s_v, 1)
+    v.memset(T.Cm[:], 0.0).then_inc(sem.s_v, 1)
+    v.memset(T.Kh[:], -0.5).then_inc(sem.s_v, 1)
+    if hk == 0:
+        v.memset(T.Kw[:], -2.0).then_inc(sem.s_v, 1)
+        v.memset(T.Cw[:], 0.0).then_inc(sem.s_v, 1)
+        n_v += 2
+    else:
+        if off > 0:
+            v.memset(T.Cw[:, 0:off], 0.0).then_inc(sem.s_v, 1)
+            n_v += 1
+        if off + F < PW:
+            v.memset(T.Cw[:, off + F:PW], 0.0).then_inc(sem.s_v, 1)
+            n_v += 1
+    v.wait_ge(sem.s_v, n_v)
+    v.wait_ge(sem.s_mw, 32)
+    n_c = 1
+    v.tensor_tensor(T.Cm[:, off:off + F], T.Mt[:], T.Km[:], AluOpType.mult).then_inc(sem.s_c, 1)
+    if hk == 0:
+        v.tensor_tensor(T.Cw[:, off:off + F], T.Wt[:], T.Kw[:], AluOpType.mult).then_inc(sem.s_c, 1)
+        n_c += 1
+    v.wait_ge(sem.s_g1, 16)
+    v.tensor_tensor(T.Z[:, HW:2 * HW], T.G[:, HW:2 * HW], T.Kh[:], AluOpType.mult).then_inc(sem.s_z, 1)
+
     n_o = 0
     if ko is not None:
-        g.scalar.dma_start(T.A[slot], T.gr[:, ko * PW:(ko + 1) * PW]).then_inc(sem.s_o, 16)
+        if ko // PH == 0:
+            g.sync.dma_start(T.A[slot], T.gr[:, ko * PW:(ko + 1) * PW]).then_inc(sem.s_o, 16)
+        else:
+            g.sync.wait_ge(sem.s_z, 1)
+            g.sync.dma_start(T.A[slot], T.Z[:, ko * PW:(ko + 1) * PW]).then_inc(sem.s_o, 16)
         n_o += 16
-    v.memset(T.K75[:], 0.75).then_inc(sem.s_v, 1)
-    v.memset(T.Km2[:], -2.0).then_inc(sem.s_v, 1)
-    v.memset(T.Cm[:], 0.0).then_inc(sem.s_v, 1)
-    v.memset(T.Cw[:], 0.0).then_inc(sem.s_v, 1)
-    v.memset(T.Kh[:], -0.5).then_inc(sem.s_v, 1)
-    v.wait_ge(sem.s_v, 5)
-    v.wait_ge(sem.s_mw, 32)
-    v.tensor_tensor(T.Cm[:, off:off + F], T.Mt[:], T.K75[:], AluOpType.mult).then_inc(sem.s_c, 1)
-    v.tensor_tensor(T.Cw[:, off:off + F], T.Wt[:], T.Km2[:], AluOpType.mult).then_inc(sem.s_c, 1)
-    if ko is not None and ko == kp:
-        g.scalar.wait_ge(sem.s_c, 2)
-        g.scalar.dma_start(T.Cd[0], T.Cm[:]).then_inc(sem.s_o, 16)
-        g.scalar.dma_start(T.Cd[1], T.Cw[:]).then_inc(sem.s_o, 16)
-        n_o += 32
+        if ko == kp:
+            g.sync.wait_ge(sem.s_c, n_c)
+            g.sync.dma_start(T.Cd[0], T.Cm[:]).then_inc(sem.s_o, 16)
+            g.sync.dma_start(T.Cd[1], T.Cw[:]).then_inc(sem.s_o, 16)
+            n_o += 32
 
-    eng = _common(topo, core, [snd[k] for k in out1])
-    order = eng[0::2] + eng[1::2]
-    seq = sorted(out1, key=lambda k: (topo.die(snd[k]) == topo.die(core), k))
-    trs = []
-    for n, k in enumerate(seq):
-        srcs = [T.G[:, k * PW:(k + 1) * PW]]
-        if k == kp:
-            srcs = srcs + [T.Cm[:], T.Cw[:]]
-        trs.append(RemoteDMATransfer(
-            dst_ids=[_dst(topo, snd[k])], dma_engine_mask=_mask(order[n * NE1:(n + 1) * NE1]), remote_sem=sem.s_a,
-            srcs=srcs, dsts=[T.A[slot]], alu_op=1 if k == kp else 0))
-    g.wait_ge(sem.s_g, 16 * len(runs))
-    g.wait_ge(sem.s_c, 2)
-    g.remote_dma_fused(trs, local_sem=sem.s_l)
-    n_l = NE1 * len(trs)
+    n_l = 0
+    for h in range(NH):
+        img = T.G if h == 0 else T.Z
+        out1 = [k for k in range(h * PH, (h + 1) * PH) if k != ko]
+        eng = _common(topo, core, [snd[k] for k in out1])
+        order = eng[0::2] + eng[1::2]
+        seq = sorted(out1, key=lambda k: (topo.die(snd[k]) == topo.die(core), k))
+        trs = []
+        for n, k in enumerate(seq):
+            srcs = [img[:, k * PW:(k + 1) * PW]]
+            if k == kp:
+                srcs = srcs + [T.Cm[:], T.Cw[:]]
+            trs.append(RemoteDMATransfer(
+                dst_ids=[_dst(topo, snd[k])], dma_engine_mask=_mask(order[n * NE1:(n + 1) * NE1]), remote_sem=sem.s_a,
+                srcs=srcs, dsts=[T.A[slot]], alu_op=1 if k == kp else 0))
+        if h == 0:
+            g.wait_ge(sem.s_g0, 16)
+        else:
+            g.wait_ge(sem.s_z, 1)
+        if kp in out1:
+            g.wait_ge(sem.s_c, n_c)
+        g.remote_dma_fused(trs, local_sem=sem.s_l)
+        n_l += NE1 * len(trs)
 
     if ko is not None:
         peers = [finishers_of(ch)[ko] for ch in others]
@@ -174,15 +215,21 @@ def rank_program(g, core, T, topo):
                               srcs=srcs, dsts=[T.B[ci]], alu_op=1)], local_sem=sem.s_l)
         n_l += 2 * NE2
 
-    v.wait_ge(sem.s_c, 2)
-    for k in range(NP):
-        v.wait_ge(s_s[k], NE3)
-        v.tensor_tensor(T.Y[:, k * PW:(k + 1) * PW], T.S[:, k * PW:(k + 1) * PW], T.Kh[:], AluOpType.mult).then_inc(sem.s_y, 1)
-        if k == kp:
-            v.tensor_tensor(T.MO[:], T.S[:, rank * F:(rank + 1) * F], T.Cw[:, off:off + F], AluOpType.subtract).then_inc(sem.s_mo, 1)
-    g.sync.wait_ge(sem.s_y, NP)
-    g.sync.dma_start(T.y[:], T.Y[:]).then_inc(sem.s_st, 16)
-    g.scalar.wait_ge(sem.s_mo, 1)
-    g.scalar.dma_start(T.mo[:], T.MO[:]).then_inc(sem.s_st, 16)
+    v.wait_ge(sem.s_c, n_c)
+    v.wait_ge(s_s[0], NE3 * PH)
+    v.tensor_tensor(T.Y[:], T.S[:, 0:HW], T.Kh[:], AluOpType.mult).then_inc(sem.s_y, 1)
+    if hk == 0:
+        v.tensor_tensor(T.MO[:], blk, T.Cw[:, off:off + F], AluOpType.subtract).then_inc(sem.s_mo, 1)
+    else:
+        v.wait_ge(s_s[1], NE3 * PH)
+        v.tensor_tensor(T.D[:], T.Cw[:, off:off + F], blk, AluOpType.subtract).then_inc(sem.s_d, 1)
+        v.wait_ge(sem.s_d, 1)
+        v.tensor_tensor(T.MO[:], T.D[:], T.D[:], AluOpType.add).then_inc(sem.s_mo, 1)
+    g.sync.wait_ge(sem.s_y, 1)
+    g.sync.dma_start(T.y[:, 0:HW], T.Y[:]).then_inc(sem.s_st, 16)
+    g.scalar.wait_ge(s_s[1], NE3 * PH)
+    g.scalar.dma_start(T.y[:, HW:2 * HW], T.S[:, HW:2 * HW]).then_inc(sem.s_st, 16)
+    g.sync.wait_ge(sem.s_mo, 1)
+    g.sync.dma_start(T.mo[:], T.MO[:]).then_inc(sem.s_st, 16)
     g.wait_ge(sem.s_l, n_l)
-    g.wait_ge(sem.s_st, 32)
+    g.wait_ge(sem.s_st, 48)

from concourse.bass import DstId, RemoteDMATransfer
from concourse.mybir import AluOpType

N = 12
F = 64
NSIM = 80
NP = 4
PW = N * F // NP
NH = 2
PH = NP // NH
HW = PW * PH
NE1 = 8
NE2 = 8
NE3 = 16

SCRATCH = {
    "G": ("sbuf", [128, N * F], "bfloat16"),
    "Z": ("sbuf", [128, N * F], "bfloat16"),
    "Mt": ("sbuf", [128, F], "bfloat16"),
    "Wt": ("sbuf", [128, F], "bfloat16"),
    "Km": ("sbuf", [128, F], "bfloat16"),
    "Kw": ("sbuf", [128, F], "bfloat16"),
    "Cm": ("sbuf", [128, PW], "bfloat16"),
    "Cw": ("sbuf", [128, PW], "bfloat16"),
    "Kh": ("psum", [128, HW], "float32"),
    "S": ("sbuf", [128, N * F], "bfloat16"),
    "Y": ("sbuf", [128, HW], "bfloat16"),
    "D": ("sbuf", [128, F], "float32"),
    "MO": ("sbuf", [128, F], "bfloat16"),
    "A": ("dram", [3, 128, PW], "bfloat16"),
    "B": ("dram", [4, 128, PW], "bfloat16"),
    "Cd": ("dram", [2, 128, PW], "bfloat16"),
}
SEMAPHORES = ["s_g0", "s_g1", "s_mw", "s_v", "s_c", "s_z", "s_a", "s_b", "s_l", "s_s0", "s_s1", "s_y", "s_d", "s_mo",
              "s_st", "s_o"]


def _bits(mask):
    return [e for e in range(16) if (mask >> e) & 1]


def _mask(engines):
    m = 0
    for e in engines:
        m |= 1 << e
    return m


def _common(topo, src, dsts):
    m = topo.mask(src, dsts[0])
    for d in dsts[1:]:
        m &= topo.mask(src, d)
    return _bits(m)


def _dst(topo, c):
    a = topo.addr(c)
    return DstId(rid=a[0], pnc=a[1])


def rank_program(g, core, T, topo):
    cores = list(T.cores)
    chips = sorted(set(topo.chip(c) for c in cores))
    my_chip = topo.chip(core)
    if my_chip not in chips:
        return
    ci = chips.index(my_chip)

    def senders_of(ch):
        ports = [c for c in range(NSIM) if topo.chip(c) == ch and all(topo.may_write(c, r) for r in cores)]
        dies = []
        for c in ports:
            if topo.die(c) not in dies:
                dies.append(topo.die(c))
        groups = [[c for c in ports if topo.die(c) == d] for d in dies]
        out = []
        for i in range(max(len(q) for q in groups)):
            for q in groups:
                if i < len(q):
                    out.append(q[i])
        return out[:NP]

    def finishers_of(ch):
        snd = senders_of(ch)
        out = []
        for c in snd:
            if T.rank_of(c) is None:
                out.append(c)
            else:
                out.append([h for h in range(NSIM) if topo.chip(h) == ch and T.rank_of(h) is None
                            and h not in snd and h not in out and topo.die(h) == topo.die(c)][0])
        return out

    snd = senders_of(my_chip)
    fin = finishers_of(my_chip)
    ranks = [c for c in cores if topo.chip(c) == my_chip]
    others = [ch for ch in chips if ch != my_chip]
    sem = T.sem
    s_s = [sem["s_s%d" % h] for h in range(NH)]
    rank = T.rank_of(core)
    mine = [T.A[j] for j in range(len(ranks))]

    def hop3(k, srcs):
        e3 = _common(topo, core, ranks)[:NE3]
        g.remote_dma_fused([RemoteDMATransfer(
            dst_ids=[_dst(topo, r) for r in ranks], dma_engine_mask=_mask(e3), remote_sem=s_s[k // PH],
            srcs=srcs, dsts=[T.S[:, k * PW:(k + 1) * PW] for r in ranks], alu_op=1)], local_sem=sem.s_l)

    if rank is None:
        if core in snd:
            k = snd.index(core)
            peers = [finishers_of(ch)[k] for ch in others]
            g.wait_ge(sem.s_a, NE1 * len(ranks))
            e2 = _common(topo, core, peers)[:NE2]
            g.remote_dma_fused([RemoteDMATransfer(
                dst_ids=[_dst(topo, p) for p in peers], dma_engine_mask=_mask(e2), remote_sem=sem.s_b,
                srcs=mine, dsts=[T.B[ci] for p in peers], alu_op=1)], local_sem=sem.s_l)
            g.wait_ge(sem.s_b, NE2 * len(peers))
            hop3(k, mine + [T.B[x] for x in range(len(chips)) if x != ci])
            g.wait_ge(sem.s_l, NE2 + NE3)
        elif core in fin:
            k = fin.index(core)
            g.wait_ge(sem.s_b, NE2 * len(chips))
            hop3(k, [T.B[x] for x in range(len(chips))])
            g.wait_ge(sem.s_l, NE3)
        return

    v = g.vector
    slot = ranks.index(core)
    kp = (rank * F) // PW
    off = rank * F - kp * PW
    hk = kp // PH
    ko = snd.index(core) if core in snd else None
    blk = T.S[:, rank * F:(rank + 1) * F]

    g.sync.dma_start(T.G[:, 0:HW], T.gr[:, 0:HW]).then_inc(sem.s_g0, 16)
    g.scalar.dma_start(T.Mt[:], T.m[:]).then_inc(sem.s_mw, 16)
    g.scalar.dma_start(T.Wt[:] if hk == 0 else T.Cw[:, off:off + F], T.w[:]).then_inc(sem.s_mw, 16)
    g.scalar.dma_start(T.G[:, HW:2 * HW], T.gr[:, HW:2 * HW]).then_inc(sem.s_g1, 16)

    n_v = 3
    v.memset(T.Km[:], 0.75 if hk == 0 else -0.375).then_inc(sem.s_v, 1)
    v.memset(T.Cm[:], 0.0).then_inc(sem.s_v, 1)
    v.memset(T.Kh[:], -0.5).then_inc(sem.s_v, 1)
    if hk == 0:
        v.memset(T.Kw[:], -2.0).then_inc(sem.s_v, 1)
        v.memset(T.Cw[:], 0.0).then_inc(sem.s_v, 1)
        n_v += 2
    else:
        if off > 0:
            v.memset(T.Cw[:, 0:off], 0.0).then_inc(sem.s_v, 1)
            n_v += 1
        if off + F < PW:
            v.memset(T.Cw[:, off + F:PW], 0.0).then_inc(sem.s_v, 1)
            n_v += 1
    v.wait_ge(sem.s_v, n_v)
    v.wait_ge(sem.s_mw, 32)
    n_c = 1
    v.tensor_tensor(T.Cm[:, off:off + F], T.Mt[:], T.Km[:], AluOpType.mult).then_inc(sem.s_c, 1)
    if hk == 0:
        v.tensor_tensor(T.Cw[:, off:off + F], T.Wt[:], T.Kw[:], AluOpType.mult).then_inc(sem.s_c, 1)
        n_c += 1
    v.wait_ge(sem.s_g1, 16)
    v.tensor_tensor(T.Z[:, HW:2 * HW], T.G[:, HW:2 * HW], T.Kh[:], AluOpType.mult).then_inc(sem.s_z, 1)

    n_o = 0
    if ko is not None:
        if ko // PH == 0:
            g.sync.dma_start(T.A[slot], T.gr[:, ko * PW:(ko + 1) * PW]).then_inc(sem.s_o, 16)
        else:
            g.sync.wait_ge(sem.s_z, 1)
            g.sync.dma_start(T.A[slot], T.Z[:, ko * PW:(ko + 1) * PW]).then_inc(sem.s_o, 16)
        n_o += 16
        if ko == kp:
            g.sync.wait_ge(sem.s_c, n_c)
            g.sync.dma_start(T.Cd[0], T.Cm[:]).then_inc(sem.s_o, 16)
            g.sync.dma_start(T.Cd[1], T.Cw[:]).then_inc(sem.s_o, 16)
            n_o += 32

    n_l = 0
    for h in range(NH):
        img = T.G if h == 0 else T.Z
        out1 = [k for k in range(h * PH, (h + 1) * PH) if k != ko]
        eng = _common(topo, core, [snd[k] for k in out1])
        order = eng[0::2] + eng[1::2]
        seq = sorted(out1, key=lambda k: (topo.die(snd[k]) == topo.die(core), k))
        trs = []
        for n, k in enumerate(seq):
            srcs = [img[:, k * PW:(k + 1) * PW]]
            if k == kp:
                srcs = srcs + [T.Cm[:], T.Cw[:]]
            trs.append(RemoteDMATransfer(
                dst_ids=[_dst(topo, snd[k])], dma_engine_mask=_mask(order[n * NE1:(n + 1) * NE1]), remote_sem=sem.s_a,
                srcs=srcs, dsts=[T.A[slot]], alu_op=1 if k == kp else 0))
        if h == 0:
            g.wait_ge(sem.s_g0, 16)
        else:
            g.wait_ge(sem.s_z, 1)
        if kp in out1:
            g.wait_ge(sem.s_c, n_c)
        g.remote_dma_fused(trs, local_sem=sem.s_l)
        n_l += NE1 * len(trs)

    if ko is not None:
        peers = [finishers_of(ch)[ko] for ch in others]
        srcs = mine + ([T.Cd[0], T.Cd[1]] if ko == kp else [])
        e_off = _common(topo, core, peers)[:NE2]
        e_on = [e for e in _bits(topo.mask(core, fin[ko])) if e not in e_off][:NE2]
        g.wait_ge(sem.s_a, NE1 * (len(ranks) - 1))
        g.wait_ge(sem.s_o, n_o)
        g.remote_dma_fused([
            RemoteDMATransfer(dst_ids=[_dst(topo, p) for p in peers], dma_engine_mask=_mask(e_off), remote_sem=sem.s_b,
                              srcs=srcs, dsts=[T.B[ci] for p in peers], alu_op=1),
            RemoteDMATransfer(dst_ids=[_dst(topo, fin[ko])], dma_engine_mask=_mask(e_on), remote_sem=sem.s_b,
                              srcs=srcs, dsts=[T.B[ci]], alu_op=1)], local_sem=sem.s_l)
        n_l += 2 * NE2

    v.wait_ge(sem.s_c, n_c)
    v.wait_ge(s_s[0], NE3 * PH)
    v.tensor_tensor(T.Y[:], T.S[:, 0:HW], T.Kh[:], AluOpType.mult).then_inc(sem.s_y, 1)
    if hk == 0:
        v.tensor_tensor(T.MO[:], blk, T.Cw[:, off:off + F], AluOpType.subtract).then_inc(sem.s_mo, 1)
    else:
        v.wait_ge(s_s[1], NE3 * PH)
        v.tensor_tensor(T.D[:], T.Cw[:, off:off + F], blk, AluOpType.subtract).then_inc(sem.s_d, 1)
        v.wait_ge(sem.s_d, 1)
        v.tensor_tensor(T.MO[:], T.D[:], T.D[:], AluOpType.add).then_inc(sem.s_mo, 1)
    g.sync.wait_ge(sem.s_y, 1)
    g.sync.dma_start(T.y[:, 0:HW], T.Y[:]).then_inc(sem.s_st, 16)
    g.scalar.wait_ge(s_s[1], NE3 * PH)
    g.scalar.dma_start(T.y[:, HW:2 * HW], T.S[:, HW:2 * HW]).then_inc(sem.s_st, 16)
    g.sync.wait_ge(sem.s_mo, 1)
    g.sync.dma_start(T.mo[:], T.MO[:]).then_inc(sem.s_st, 16)
    g.wait_ge(sem.s_l, n_l)
    g.wait_ge(sem.s_st, 48)
